import numpy as np
import ml_dtypes


def mxq(x, axis, fmt="e4m3"):
    dtype, down = {"e4m3": (ml_dtypes.float8_e4m3fn, 7), "e5m2": (ml_dtypes.float8_e5m2, 14)}[fmt]
    v = np.moveaxis(np.asarray(x, np.float32).astype(ml_dtypes.bfloat16).astype(np.float64), axis, -1)
    blocks = v.reshape(v.shape[:-1] + (-1, 32))
    amax = np.abs(blocks).max(-1, keepdims=True)
    byte = np.maximum(np.where(amax > 0, np.frexp(amax)[1] - 1 + 127, 0) - down, 1)
    scale = np.exp2(byte - 127.0)
    codes = (blocks / scale).astype(np.float32).astype(dtype).astype(np.float64)
    return np.moveaxis((codes * scale).reshape(v.shape), -1, axis)


WIDE = False


def mx_kscale(k):
    if not WIDE:
        return np.ones(k)
    levels = np.array([10, -10, 5, -5, 0])
    if k % 512:
        return np.exp2(np.random.permutation(np.resize(levels, k // 32))).repeat(32)
    a = np.empty((k // 512, 16))
    for p in range(k // 512):
        a[p, :8] = np.random.permutation(np.resize(levels, 8))
        for g in range(8):
            far = levels[np.abs(levels - a[p, g]) >= 10]
            a[p, g + 8] = far[np.random.randint(len(far))]
    return np.exp2(a.ravel()).repeat(32)


def f64(x):
    return np.asarray(x).astype(np.float64)


def striped(idx):
    return np.tile(idx.reshape(-1, 16).T, (8, 1)).astype(np.uint16)


def unstriped(offs):
    return offs[:16].T.reshape(-1).astype(np.int64)


def striped8(idx):
    return np.concatenate([x.reshape(-1, 16).T for x in idx]).astype(np.uint16)


def runs(offs, k):
    lists = np.stack([offs[16 * r : 16 * r + 16].T.reshape(-1) for r in range(8)]).astype(np.int64)
    return lists[np.arange(k) % 512 // 64]


def pack_weight(w):
    k, n = w.shape
    w = f64(np.asarray(w, np.float32).astype(ml_dtypes.bfloat16)).reshape(k // 32, 32, n)
    amax = np.abs(w).max(1)
    byte = np.clip(np.where(amax > 0, np.frexp(amax)[1] - 1 + 127 - 7, 1), 1, 254)
    scaled = (w * np.exp2(127.0 - byte)[:, None, :]).reshape(k, n).astype(np.float32)
    words = np.ascontiguousarray(scaled.reshape(k // 512, 128, 4, n).transpose(0, 1, 3, 2)).astype(ml_dtypes.float8_e4m3fn).view(np.uint8)
    return words, np.ascontiguousarray(byte.astype(np.uint8).reshape(k // 512, 16, n))


def unpack_weight(words, scales):
    g, p, n, _ = words.shape
    vals = np.ascontiguousarray(words).view(ml_dtypes.float8_e4m3fn).astype(np.float64) * np.repeat(np.exp2(scales.astype(np.float64) - 127.0), 8, axis=1)[..., None]
    return vals.transpose(0, 1, 3, 2).reshape(g * 512, n)


K, T, S, H, C = 512, 2048, 512, 512, 512


def setup_inputs():
    n = np.random.standard_normal
    s = mx_kscale(K)[:, None]
    packed_xT = pack_weight(n((K, T)) * s)
    return {
        "x_words": packed_xT[0],
        "x_scales": packed_xT[1],
        "w1": (n((K, H)) / np.sqrt(K) / s).astype(np.float32),
        "gs": (np.random.uniform(0.5, 1.5, (K, 1)) / s).astype(np.float32),
        "offs": striped(np.random.permutation(T)[:S]),
        "n1": striped8(np.stack([np.random.permutation(S) for _ in range(8)])),
        "n2": striped8(np.stack([np.random.permutation(S) for _ in range(8)])),
        "n3": striped8(np.stack([np.random.permutation(S) for _ in range(8)])),
        "ca": striped(np.random.permutation(T)[:C]),
        "cb": striped(np.random.permutation(T)[:C]),
        "n4": striped8(np.stack([np.random.permutation(S) for _ in range(8)])),
        "n5": striped8(np.stack([np.random.permutation(S) for _ in range(8)])),
        "n6": striped8(np.stack([np.random.permutation(S) for _ in range(8)])),
    }


def reference(x_words, x_scales, w1, gs, offs, n1, n2, n3, ca, cb, n4, n5, n6):
    x_ca = unpack_weight(x_words, x_scales)[:, unstriped(ca)]
    xq = unpack_weight(x_words, x_scales)[:, unstriped(offs)]
    y = mxq(f64(w1), 0, "e4m3").T @ xq
    z = f64(gs) * (y + y[np.arange(H)[:, None], runs(n1, H)] - (np.maximum(y[np.arange(H)[:, None], runs(n2, H)], y[np.arange(H)[:, None], runs(n3, H)])))
    zq = mxq(z, 0, "e4m3")
    a = 0.0625 * (x_ca.T @ zq)
    x_cb = unpack_weight(x_words, x_scales)[:, unstriped(cb)]
    b = 0.0625 * (x_cb.T @ zq)
    return np.maximum(np.minimum(a - (0.5 * (a[np.arange(C)[:, None], runs(n4, C)])), b[np.arange(C)[:, None], runs(n5, C)]), b[np.arange(C)[:, None], runs(n6, C)])

@@ -1,0 +1,251 @@
+from contextlib import ExitStack
+
+import concourse.mybir as mybir
+
+K, T, S, H, C = 512, 2048, 512, 512, 512
+FLOPS = 2 * K * S * (H + 2 * C)
+
+F32 = mybir.dt.float32
+BF16 = mybir.dt.bfloat16
+I32 = mybir.dt.int32
+U32 = mybir.dt.uint32
+U16 = mybir.dt.uint16
+U8 = mybir.dt.uint8
+FP8X4 = mybir.dt.float8_e4m3fn_x4
+ALU = mybir.AluOpType
+COPY = mybir.ActivationFunctionType.Copy
+
+P = 128
+PACK = 4
+HALF = S // 2
+WINDOW = 2 * S
+ALL = slice(0, S)
+HALVES = (slice(0, HALF), slice(HALF, S))
+
+
+def entries(cols):
+    return slice(cols.start // 16, cols.stop // 16)
+
+
+def spare(cols):
+    return slice(S + cols.start, S + cols.stop)
+
+
+def tile_picked_ccmpclampbtrim_none_p_kernel(
+    tc, x_words, x_scales, w1, gs, offs, n1, n2, n3, ca, cb, n4, n5, n6, out
+):
+    nc = tc.nc
+    with ExitStack() as ctx:
+        held = ctx.enter_context(tc.tile_pool(name="held", bufs=1))
+        psum = ctx.enter_context(tc.psum_pool(name="psum", bufs=1))
+
+        def load_list(name, src):
+            tile = held.tile([P, S // 16], U16, name=name)
+            nc.sync.dma_start(tile[:], src)
+            return tile
+
+        table_scales = held.tile([P, T], U8, name="table_scales")
+        nc.gpsimd.memset(table_scales[:].bitcast(I32), 0)
+        for q in range(4):
+            nc.scalar.dma_start(
+                table_scales[32 * q : 32 * q + 4, :].bitcast(I32), x_scales[0, 4 * q : 4 * q + 4, :].bitcast(I32)
+            )
+        w_rows = w1.rearrange("(p j) c -> p j c", j=PACK)
+        w_raw = [held.tile([P, PACK, H // 2], F32, name="w_raw%d" % u) for u in range(2)]
+        nc.sync.dma_start(w_raw[0][:], w_rows[:, :, 0 : H // 2])
+        offs_t = load_list("offs_t", offs)
+        nc.sync.dma_start(w_raw[1][:], w_rows[:, :, H // 2 : H])
+        table_words = held.tile([P, T], U32, name="table_words")
+        nc.sync.dma_start(table_words[:].bitcast(I32), x_words[0].rearrange("p n r -> p (n r)").bitcast(I32))
+        ca_t = load_list("ca_t", ca)
+        cb_t = load_list("cb_t", cb)
+        n1_t = load_list("n1_t", n1)
+        n2_t = load_list("n2_t", n2)
+        n3_t = load_list("n3_t", n3)
+        gain = held.tile([P, PACK], F32, name="gain")
+        nc.sync.dma_start(gain[:], gs.rearrange("(p t) o -> p (t o)", t=PACK))
+        n4_t = load_list("n4_t", n4)
+        n5_t = load_list("n5_t", n5)
+        n6_t = load_list("n6_t", n6)
+
+        y_win = [held.tile([P, WINDOW], F32, name="y_win%d" % t) for t in range(PACK)]
+        a_win = [held.tile([P, WINDOW], F32, name="a_win%d" % t) for t in range(PACK)]
+        b_win = [held.tile([P, WINDOW], F32, name="b_win%d" % t) for t in range(PACK)]
+        for t in range(PACK):
+            nc.gpsimd.memset(y_win[t][:, spare(ALL)], 0.0)
+
+        def gather_scales(name, lst):
+            tile = held.tile([P, S], U8, name=name, align_bytes=64)
+            nc.vector.tensor_copy(tile[:], table_scales[:].indirect(lst[:]))
+            return tile
+
+        def deal_scales(name, src):
+            tile = held.tile([P, S], U8, name=name, align_bytes=64)
+            nc.vector.tensor_copy(
+                tile[:].bitcast(I32).rearrange("p (t c) -> p t c", t=PACK),
+                src[:].bitcast(I32).rearrange("p (c t) -> p t c", t=PACK),
+            )
+            return tile
+
+        def gather_dealt_words(tile, lst):
+            nc.vector.tensor_copy(
+                tile[:].rearrange("p (t c b) -> p c t b", t=PACK, b=4), table_words[:].indirect(lst[:])
+            )
+
+        xq_scales = gather_scales("xq_scales", offs_t)
+        ca_plain = gather_scales("ca_plain", ca_t)
+        cb_plain = gather_scales("cb_plain", cb_t)
+
+        w_bf = held.tile([P, H * PACK], BF16, name="w_bf", align_bytes=64)
+        w_view = w_bf[:].rearrange("p (t m j) -> p m t j", t=PACK, j=PACK)
+        for u in range(2):
+            nc.scalar.copy(w_view[:, 64 * u : 64 * (u + 1)], w_raw[u][:].rearrange("p j (m t) -> p m t j", t=PACK))
+        w_codes = held.tile([P, H], U32, name="w_codes", align_bytes=64)
+        w_scales = held.tile([P, H], U8, name="w_scales", align_bytes=64)
+        nc.vector.quantize_mx(out=w_codes[:].bitcast(FP8X4), scales=w_scales[:], in_=w_bf[:])
+
+        xq_words = held.tile([P, S], U32, name="xq_words", align_bytes=64)
+        nc.vector.tensor_copy(xq_words[:], table_words[:].indirect(offs_t[:]))
+        ca_scales = deal_scales("ca_scales", ca_plain)
+        cb_scales = deal_scales("cb_scales", cb_plain)
+        ca_words = held.tile([P, C], U32, name="ca_words", align_bytes=64)
+        gather_dealt_words(ca_words, ca_t)
+
+        def product(bank, cols, left_words, left_scales, t, right_words, right_scales):
+            rows = slice(P * t, P * (t + 1))
+            nc.tensor.matmul_mx(
+                out=bank[:, cols],
+                lhsT=left_words[:, rows].bitcast(FP8X4),
+                lhsT_scale=left_scales[:, rows],
+                rhs=right_words[:, cols].bitcast(FP8X4),
+                rhs_scale=right_scales[:, cols],
+                start=True,
+                stop=True,
+            )
+
+        for t in range(PACK):
+            bank = psum.tile([P, S], F32, name="y_bank%d" % t, tag="yb%d" % t)
+            product(bank, ALL, w_codes, w_scales, t, xq_words, xq_scales)
+            nc.scalar.activation(y_win[t][:, ALL], bank[:], COPY, scale=-1.0)
+            nc.scalar.activation(a_win[t][:, spare(ALL)], bank[:], COPY, scale=-1.0)
+
+        pair_sum = [held.tile([P, S], F32, name="pair_sum%d" % t) for t in range(PACK)]
+        less2 = [held.tile([P, S], F32, name="less2_%d" % t) for t in range(PACK)]
+        less3 = [held.tile([P, S], F32, name="less3_%d" % t, tag="l3_%d" % t, align_bytes=64) for t in range(PACK)]
+        least = [held.tile([P, S], F32, name="least%d" % t) for t in range(PACK)]
+        z_bf = held.tile([P, S, PACK], BF16, name="z_bf", align_bytes=64)
+        z_codes = held.tile([P, S], U32, name="z_codes", align_bytes=64)
+        z_scales = held.tile([P, S], U8, name="z_scales", align_bytes=64)
+
+        def fetch1(t):
+            nc.vector.tensor_tensor(pair_sum[t][:], y_win[t][:].indirect(n1_t[:]), a_win[t][:, spare(ALL)], ALU.add)
+
+        def fetch2(t, cols):
+            nc.vector.tensor_tensor(
+                less2[t][:, cols], y_win[t][:].indirect(n2_t[:, entries(cols)]), pair_sum[t][:, cols], ALU.subtract
+            )
+
+        def fetch3(t, cols):
+            nc.vector.tensor_tensor(
+                less3[t][:, cols], y_win[t][:].indirect(n3_t[:, entries(cols)]), pair_sum[t][:, cols], ALU.subtract
+            )
+
+        def make_z(t, cols):
+            nc.vector.tensor_tensor(least[t][:, cols], less2[t][:, cols], less3[t][:, cols], ALU.min)
+            nc.scalar.activation(z_bf[:, cols, t], least[t][:, cols], COPY, scale=gain[:, t : t + 1])
+
+        def quantize_z(cols):
+            nc.vector.quantize_mx(
+                out=z_codes[:, cols].bitcast(FP8X4),
+                scales=z_scales[:, cols],
+                in_=z_bf[:, cols, :].rearrange("p c t -> p (c t)"),
+            )
+
+        a_bank = [psum.tile([P, S], F32, name="a_bank%d" % t) for t in range(PACK)]
+
+        def make_a(t, cols):
+            product(a_bank[t], cols, ca_words, ca_scales, t, z_codes, z_scales)
+            nc.scalar.activation(a_win[t][:, cols], a_bank[t][:, cols], COPY, scale=-0.03125)
+            nc.scalar.activation(b_win[t][:, spare(cols)], a_bank[t][:, cols], COPY, scale=0.0625)
+
+        def make_b(t):
+            bank = psum.tile([P, S], F32, name="b_bank%d" % t, tag="yb%d" % t)
+            product(bank, ALL, cb_words, cb_scales, t, z_codes, z_scales)
+            nc.scalar.activation(b_win[t][:, ALL], bank[:], COPY, scale=0.0625)
+
+        first, second = HALVES
+        fetch1(0)
+        fetch1(1)
+        fetch2(0, ALL)
+        fetch3(0, ALL)
+        fetch2(1, ALL)
+        make_z(0, ALL)
+        fetch3(1, ALL)
+        fetch1(2)
+        make_z(1, ALL)
+        fetch1(3)
+        fetch2(2, first)
+        fetch3(2, first)
+        fetch2(3, first)
+        make_z(2, first)
+        fetch3(3, first)
+        fetch2(2, second)
+        make_z(3, first)
+        fetch3(2, second)
+        fetch2(3, second)
+        make_z(2, second)
+        fetch3(3, second)
+        quantize_z(first)
+        make_z(3, second)
+        make_a(0, first)
+        cb_words = held.tile([P, C], U32, name="cb_words", tag="l3_3", align_bytes=64)
+        gather_dealt_words(cb_words, cb_t)
+        quantize_z(second)
+
+        make_a(0, second)
+        make_a(1, ALL)
+        make_b(0)
+        make_b(1)
+        for t in range(2, PACK):
+            make_a(t, ALL)
+            make_b(t)
+
+        trimmed = [held.tile([P, S], F32, name="trimmed%d" % t) for t in range(PACK)]
+        upper = [held.tile([P, S], F32, name="upper%d" % t) for t in range(PACK)]
+        lower = [held.tile([P, S], F32, name="lower%d" % t) for t in range(PACK)]
+        capped = [held.tile([P, S], F32, name="capped%d" % t) for t in range(PACK)]
+        result = [held.tile([P, S], F32, name="result%d" % t) for t in range(PACK)]
+        out_rows = out.rearrange("(c t b) j -> t c b j", t=PACK, b=4)
+
+        def fetch4(t):
+            nc.vector.tensor_tensor(trimmed[t][:], a_win[t][:].indirect(n4_t[:]), b_win[t][:, spare(ALL)], ALU.add)
+
+        def fetch5(t):
+            nc.vector.tensor_copy(upper[t][:], b_win[t][:].indirect(n5_t[:]))
+
+        def fetch6(t, cols):
+            nc.vector.tensor_copy(lower[t][:, cols], b_win[t][:].indirect(n6_t[:, entries(cols)]))
+
+        def cap(t):
+            nc.vector.tensor_tensor(capped[t][:], trimmed[t][:], upper[t][:], ALU.min)
+
+        def finish(t, cols):
+            nc.vector.tensor_tensor(result[t][:, cols], capped[t][:, cols], lower[t][:, cols], ALU.max)
+            nc.sync.dma_start(out_rows[t][:, :, cols], result[t][:, cols])
+
+        fetch4(0)
+        for t in range(PACK - 1):
+            fetch4(t + 1)
+            fetch5(t)
+            fetch6(t, ALL)
+            cap(t)
+            if t > 0:
+                finish(t - 1, ALL)
+        last = PACK - 1
+        fetch5(last)
+        finish(last - 1, ALL)
+        fetch6(last, first)
+        cap(last)
+        fetch6(last, second)
+        finish(last, first)
+        finish(last, second)

@@ -1,6 +1,7 @@
 from contextlib import ExitStack
 
 import concourse.mybir as mybir
+from concourse.masks import make_identity
 
 K, T, S, H, C = 512, 2048, 512, 512, 512
 FLOPS = 2 * K * S * (H + 2 * C)
@@ -46,19 +47,17 @@ def tile_picked_ccmpclampbtrim_none_p_kernel(
 
         table_scales = held.tile([P, T], U8, name="table_scales")
         nc.gpsimd.memset(table_scales[:].bitcast(I32), 0)
-        for q in range(4):
-            nc.scalar.dma_start(
-                table_scales[32 * q : 32 * q + 4, :].bitcast(I32), x_scales[0, 4 * q : 4 * q + 4, :].bitcast(I32)
-            )
-        w_rows = w1.rearrange("(p j) c -> p j c", j=PACK)
-        w_raw = [held.tile([P, PACK, H // 2], F32, name="w_raw%d" % u) for u in range(2)]
-        nc.sync.dma_start(w_raw[0][:], w_rows[:, :, 0 : H // 2])
         offs_t = load_list("offs_t", offs)
-        nc.sync.dma_start(w_raw[1][:], w_rows[:, :, H // 2 : H])
-        table_words = held.tile([P, T], U32, name="table_words")
-        nc.sync.dma_start(table_words[:].bitcast(I32), x_words[0].rearrange("p n r -> p (n r)").bitcast(I32))
         ca_t = load_list("ca_t", ca)
         cb_t = load_list("cb_t", cb)
+        for q in range(4):
+            nc.sync.dma_start(
+                table_scales[32 * q : 32 * q + 4, :].bitcast(I32), x_scales[0, 4 * q : 4 * q + 4, :].bitcast(I32)
+            )
+        w_raw = held.tile([P, PACK, H], F32, name="w_raw")
+        nc.sync.dma_start(w_raw[:], w1.rearrange("(p j) c -> p j c", j=PACK))
+        table_words = held.tile([P, T], U32, name="table_words")
+        nc.sync.dma_start(table_words[:].bitcast(I32), x_words[0].rearrange("p n r -> p (n r)").bitcast(I32))
         n1_t = load_list("n1_t", n1)
         n2_t = load_list("n2_t", n2)
         n3_t = load_list("n3_t", n3)
@@ -68,48 +67,63 @@ def tile_picked_ccmpclampbtrim_none_p_kernel(
         n5_t = load_list("n5_t", n5)
         n6_t = load_list("n6_t", n6)
 
-        y_win = [held.tile([P, WINDOW], F32, name="y_win%d" % t) for t in range(PACK)]
+        last = PACK - 1
+        y_win = [held.tile([P, WINDOW if t < last else S], F32, name="y_win%d" % t) for t in range(PACK)]
         a_win = [held.tile([P, WINDOW], F32, name="a_win%d" % t) for t in range(PACK)]
         b_win = [held.tile([P, WINDOW], F32, name="b_win%d" % t) for t in range(PACK)]
-        for t in range(PACK):
+        for t in range(last):
             nc.gpsimd.memset(y_win[t][:, spare(ALL)], 0.0)
 
-        def gather_scales(name, lst):
-            tile = held.tile([P, S], U8, name=name, align_bytes=64)
-            nc.vector.tensor_copy(tile[:], table_scales[:].indirect(lst[:]))
-            return tile
+        identity = held.tile([P, P], F32, name="identity")
+        make_identity(nc, identity[:])
 
-        def deal_scales(name, src):
-            tile = held.tile([P, S], U8, name=name, align_bytes=64)
+        def gather_scales(tile, lst, cols):
+            nc.vector.tensor_copy(tile[:], table_scales[:].indirect(lst[:, entries(cols)]))
+
+        def deal_scales(tile, cols, src):
             nc.vector.tensor_copy(
-                tile[:].bitcast(I32).rearrange("p (t c) -> p t c", t=PACK),
+                tile[:].bitcast(I32).rearrange("p (t c) -> p t c", t=PACK)[:, :, entries(cols)],
                 src[:].bitcast(I32).rearrange("p (c t) -> p t c", t=PACK),
             )
-            return tile
 
         def gather_dealt_words(tile, lst):
             nc.vector.tensor_copy(
                 tile[:].rearrange("p (t c b) -> p c t b", t=PACK, b=4), table_words[:].indirect(lst[:])
             )
 
-        xq_scales = gather_scales("xq_scales", offs_t)
-        ca_plain = gather_scales("ca_plain", ca_t)
-        cb_plain = gather_scales("cb_plain", cb_t)
+        first, second = HALVES
+        xq_scales = held.tile([P, S], U8, name="xq_scales", align_bytes=64)
+        gather_scales(xq_scales, offs_t, ALL)
+        ca_plain = held.tile([P, C], U8, name="ca_plain")
+        gather_scales(ca_plain, ca_t, ALL)
+        cb_early = held.tile([P, HALF], U8, name="cb_early")
+        gather_scales(cb_early, cb_t, first)
+        ca_scales = held.tile([P, C], U8, name="ca_scales", align_bytes=64)
+        cb_scales = held.tile([P, C], U8, name="cb_scales", align_bytes=64)
+        deal_scales(ca_scales, ALL, ca_plain)
+        deal_scales(cb_scales, first, cb_early)
 
-        w_bf = held.tile([P, H * PACK], BF16, name="w_bf", align_bytes=64)
-        w_view = w_bf[:].rearrange("p (t m j) -> p m t j", t=PACK, j=PACK)
-        for u in range(2):
-            nc.scalar.copy(w_view[:, 64 * u : 64 * (u + 1)], w_raw[u][:].rearrange("p j (m t) -> p m t j", t=PACK))
+        raw_view = w_raw[:].rearrange("p j (m t) -> p m t j", t=PACK)
         w_codes = held.tile([P, H], U32, name="w_codes", align_bytes=64)
         w_scales = held.tile([P, H], U8, name="w_scales", align_bytes=64)
-        nc.vector.quantize_mx(out=w_codes[:].bitcast(FP8X4), scales=w_scales[:], in_=w_bf[:])
+        w_bf = [held.tile([P, 2 * H], BF16, name="w_bf%d" % u, tag="w_bf%d" % u, align_bytes=64) for u in range(2)]
+        w_view = [tile[:].rearrange("p (t m j) -> p m t j", t=2, j=PACK) for tile in w_bf]
+        nc.scalar.copy(w_view[0], raw_view[:, :, 0:2])
+        nc.scalar.copy(w_view[1], raw_view[:, :, 2:4])
+        for u, cols in enumerate(HALVES):
+            nc.vector.quantize_mx(out=w_codes[:, cols].bitcast(FP8X4), scales=w_scales[:, cols], in_=w_bf[u][:])
 
-        xq_words = held.tile([P, S], U32, name="xq_words", align_bytes=64)
-        nc.vector.tensor_copy(xq_words[:], table_words[:].indirect(offs_t[:]))
-        ca_scales = deal_scales("ca_scales", ca_plain)
-        cb_scales = deal_scales("cb_scales", cb_plain)
-        ca_words = held.tile([P, C], U32, name="ca_words", align_bytes=64)
+        xq_words = held.tile([P, S], U32, name="xq_words", tag="w_bf0", align_bytes=64)
+        for cols in HALVES:
+            nc.vector.tensor_copy(xq_words[:, cols], table_words[:].indirect(offs_t[:, entries(cols)]))
+        ca_words = held.tile([P, C], U32, name="ca_words", tag="w_bf1", align_bytes=64)
         gather_dealt_words(ca_words, ca_t)
+
+        turn = [0]
+
+        def next_bank():
+            turn.append(turn[-1] + 1)
+            return psum.tile([P, S], F32, name="bank%d" % turn[-1], tag="bank%d" % (turn[-1] % 8))
 
         def product(bank, cols, left_words, left_scales, t, right_words, right_scales):
             rows = slice(P * t, P * (t + 1))
@@ -123,22 +137,30 @@ def tile_picked_ccmpclampbtrim_none_p_kernel(
                 stop=True,
             )
 
-        for t in range(PACK):
-            bank = psum.tile([P, S], F32, name="y_bank%d" % t, tag="yb%d" % t)
-            product(bank, ALL, w_codes, w_scales, t, xq_words, xq_scales)
-            nc.scalar.activation(y_win[t][:, ALL], bank[:], COPY, scale=-1.0)
-            nc.scalar.activation(a_win[t][:, spare(ALL)], bank[:], COPY, scale=-1.0)
+        def make_y(t, cols):
+            bank = next_bank()
+            product(bank, cols, w_codes, w_scales, t, xq_words, xq_scales)
+            nc.scalar.activation(y_win[t][:, cols], bank[:, cols], COPY, scale=-1.0)
+            nc.scalar.activation(a_win[t][:, spare(cols)], bank[:, cols], COPY, scale=-1.0)
 
-        pair_sum = [held.tile([P, S], F32, name="pair_sum%d" % t) for t in range(PACK)]
+        make_y(0, first)
+        make_y(0, second)
+        for t in range(1, PACK):
+            make_y(t, ALL)
+
+        third, fourth = slice(HALF, HALF + P), slice(HALF + P, S)
+        pair_sum = [held.tile([P, S], F32, name="pair_sum%d" % t, tag="pair_sum%d" % t) for t in range(PACK)]
         less2 = [held.tile([P, S], F32, name="less2_%d" % t) for t in range(PACK)]
-        less3 = [held.tile([P, S], F32, name="less3_%d" % t, tag="l3_%d" % t, align_bytes=64) for t in range(PACK)]
-        least = [held.tile([P, S], F32, name="least%d" % t) for t in range(PACK)]
+        less3 = [held.tile([P, S], F32, name="less3_%d" % t) for t in range(PACK)]
+        least = [held.tile([P, S], F32, name="least%d" % t, tag="least%d" % t, align_bytes=64) for t in range(PACK)]
         z_bf = held.tile([P, S, PACK], BF16, name="z_bf", align_bytes=64)
         z_codes = held.tile([P, S], U32, name="z_codes", align_bytes=64)
         z_scales = held.tile([P, S], U8, name="z_scales", align_bytes=64)
 
-        def fetch1(t):
-            nc.vector.tensor_tensor(pair_sum[t][:], y_win[t][:].indirect(n1_t[:]), a_win[t][:, spare(ALL)], ALU.add)
+        def fetch1(t, cols):
+            nc.vector.tensor_tensor(
+                pair_sum[t][:, cols], y_win[t][:].indirect(n1_t[:, entries(cols)]), a_win[t][:, spare(cols)], ALU.add
+            )
 
         def fetch2(t, cols):
             nc.vector.tensor_tensor(
@@ -161,48 +183,52 @@ def tile_picked_ccmpclampbtrim_none_p_kernel(
                 in_=z_bf[:, cols, :].rearrange("p c t -> p (c t)"),
             )
 
-        a_bank = [psum.tile([P, S], F32, name="a_bank%d" % t) for t in range(PACK)]
-
         def make_a(t, cols):
-            product(a_bank[t], cols, ca_words, ca_scales, t, z_codes, z_scales)
-            nc.scalar.activation(a_win[t][:, cols], a_bank[t][:, cols], COPY, scale=-0.03125)
-            nc.scalar.activation(b_win[t][:, spare(cols)], a_bank[t][:, cols], COPY, scale=0.0625)
+            bank = next_bank()
+            product(bank, cols, ca_words, ca_scales, t, z_codes, z_scales)
+            nc.scalar.activation(a_win[t][:, cols], bank[:, cols], COPY, scale=-0.03125)
+            nc.scalar.activation(b_win[t][:, spare(cols)], bank[:, cols], COPY, scale=0.0625)
 
         def make_b(t):
-            bank = psum.tile([P, S], F32, name="b_bank%d" % t, tag="yb%d" % t)
+            bank = next_bank()
             product(bank, ALL, cb_words, cb_scales, t, z_codes, z_scales)
             nc.scalar.activation(b_win[t][:, ALL], bank[:], COPY, scale=0.0625)
 
-        first, second = HALVES
-        fetch1(0)
-        fetch1(1)
+        fetch1(0, ALL)
+        fetch1(1, ALL)
         fetch2(0, ALL)
         fetch3(0, ALL)
         fetch2(1, ALL)
         make_z(0, ALL)
         fetch3(1, ALL)
-        fetch1(2)
+        fetch1(2, ALL)
         make_z(1, ALL)
-        fetch1(3)
-        fetch2(2, first)
-        fetch3(2, first)
+        fetch2(2, ALL)
+        fetch1(3, first)
+        fetch3(2, ALL)
+        fetch1(3, second)
+        make_z(2, ALL)
         fetch2(3, first)
-        make_z(2, first)
         fetch3(3, first)
-        fetch2(2, second)
+        fetch2(3, third)
         make_z(3, first)
-        fetch3(2, second)
-        fetch2(3, second)
-        make_z(2, second)
-        fetch3(3, second)
+        fetch3(3, third)
+        fetch2(3, fourth)
+        make_z(3, third)
+        fetch3(3, fourth)
         quantize_z(first)
-        make_z(3, second)
+        make_z(3, fourth)
         make_a(0, first)
-        cb_words = held.tile([P, C], U32, name="cb_words", tag="l3_3", align_bytes=64)
+        quantize_z(third)
+        cb_late = held.tile([P, HALF], U8, name="cb_late", tag="pair_sum%d" % last)
+        gather_scales(cb_late, cb_t, second)
+        make_a(0, third)
+        quantize_z(fourth)
+        cb_words = held.tile([P, C], U32, name="cb_words", tag="least%d" % last, align_bytes=64)
         gather_dealt_words(cb_words, cb_t)
-        quantize_z(second)
+        deal_scales(cb_scales, second, cb_late)
 
-        make_a(0, second)
+        make_a(0, fourth)
         make_a(1, ALL)
         make_b(0)
         make_b(1)
@@ -214,38 +240,57 @@ def tile_picked_ccmpclampbtrim_none_p_kernel(
         upper = [held.tile([P, S], F32, name="upper%d" % t) for t in range(PACK)]
         lower = [held.tile([P, S], F32, name="lower%d" % t) for t in range(PACK)]
         capped = [held.tile([P, S], F32, name="capped%d" % t) for t in range(PACK)]
+        turned = [held.tile([P, S], F32, name="turned%d" % t) for t in range(last)]
         result = [held.tile([P, S], F32, name="result%d" % t) for t in range(PACK)]
         out_rows = out.rearrange("(c t b) j -> t c b j", t=PACK, b=4)
 
         def fetch4(t):
             nc.vector.tensor_tensor(trimmed[t][:], a_win[t][:].indirect(n4_t[:]), b_win[t][:, spare(ALL)], ALU.add)
 
-        def fetch5(t):
-            nc.vector.tensor_copy(upper[t][:], b_win[t][:].indirect(n5_t[:]))
+        def room(t, dst, lst, cols):
+            nc.vector.tensor_tensor(
+                dst[t][:, cols], b_win[t][:].indirect(lst[:, entries(cols)]), trimmed[t][:, cols], ALU.subtract
+            )
 
-        def fetch6(t, cols):
-            nc.vector.tensor_copy(lower[t][:, cols], b_win[t][:].indirect(n6_t[:, entries(cols)]))
+        def shift_and_store(t, cols):
+            nc.vector.scalar_tensor_tensor(
+                capped[t][:, cols], upper[t][:, cols], 0.0, lower[t][:, cols], ALU.min, ALU.max
+            )
+            blocks = [slice(q, q + P) for q in range(cols.start, cols.stop, P)]
+            there = next_bank()
+            for blk in blocks:
+                nc.tensor.matmul(there[:, blk], trimmed[t][:, blk], identity[:], start=True, stop=False, is_transpose=True)
+                nc.tensor.matmul(there[:, blk], capped[t][:, blk], identity[:], start=False, stop=True, is_transpose=True)
+            nc.scalar.copy(turned[t][:, cols], there[:, cols])
+            back = next_bank()
+            for blk in blocks:
+                nc.tensor.transpose(back[:, blk], turned[t][:, blk], identity[:])
+            nc.scalar.copy(result[t][:, cols], back[:, cols])
+            nc.scalar.dma_start(out_rows[t][:, :, cols], result[t][:, cols])
 
-        def cap(t):
-            nc.vector.tensor_tensor(capped[t][:], trimmed[t][:], upper[t][:], ALU.min)
-
-        def finish(t, cols):
-            nc.vector.tensor_tensor(result[t][:, cols], capped[t][:, cols], lower[t][:, cols], ALU.max)
-            nc.sync.dma_start(out_rows[t][:, :, cols], result[t][:, cols])
+        def fetch(dst, lst, cols):
+            nc.vector.tensor_copy(dst[last][:, cols], b_win[last][:].indirect(lst[:, entries(cols)]))
 
         fetch4(0)
-        for t in range(PACK - 1):
-            fetch4(t + 1)
-            fetch5(t)
-            fetch6(t, ALL)
-            cap(t)
-            if t > 0:
-                finish(t - 1, ALL)
-        last = PACK - 1
-        fetch5(last)
-        finish(last - 1, ALL)
-        fetch6(last, first)
-        cap(last)
-        fetch6(last, second)
-        finish(last, first)
-        finish(last, second)
+        fetch4(1)
+        room(0, upper, n5_t, ALL)
+        room(0, lower, n6_t, ALL)
+        room(1, upper, n5_t, ALL)
+        shift_and_store(0, ALL)
+        room(1, lower, n6_t, ALL)
+        fetch4(2)
+        shift_and_store(1, ALL)
+        room(2, upper, n5_t, ALL)
+        for cols in HALVES:
+            room(2, lower, n6_t, cols)
+        for cols in HALVES:
+            shift_and_store(2, cols)
+        fetch4(last)
+        fetch(lower, n6_t, ALL)
+        for cols in HALVES:
+            fetch(upper, n5_t, cols)
+        for cols in HALVES:
+            nc.vector.tensor_tensor(capped[last][:, cols], trimmed[last][:, cols], upper[last][:, cols], ALU.min)
+        for cols in HALVES:
+            nc.vector.tensor_tensor(result[last][:, cols], capped[last][:, cols], lower[last][:, cols], ALU.max)
+            nc.sync.dma_start(out_rows[last][:, :, cols], result[last][:, cols])

@@ -14,6 +14,7 @@ U16 = mybir.dt.uint16
 U8 = mybir.dt.uint8
 FP8X4 = mybir.dt.float8_e4m3fn_x4
 ALU = mybir.AluOpType
+RELU = mybir.ActivationFunctionType.Relu
 COPY = mybir.ActivationFunctionType.Copy
 
 P = 128
@@ -52,14 +53,14 @@ def tile_picked_ccmpclampbtrim_none_p_kernel(
         cb_t = load_list("cb_t", cb)
         for q in range(4):
             nc.sync.dma_start(
-                table_scales[32 * q : 32 * q + 4, :].bitcast(I32), x_scales[0, 4 * q : 4 * q + 4, :].bitcast(I32)
+                table_scales[q:P:32, :].bitcast(I32), x_scales[0, q:16:4, :].bitcast(I32)
             )
         w_raw = held.tile([P, PACK, H], F32, name="w_raw")
         nc.sync.dma_start(w_raw[:], w1.rearrange("(p j) c -> p j c", j=PACK))
         table_words = held.tile([P, T], U32, name="table_words")
         nc.sync.dma_start(table_words[:].bitcast(I32), x_words[0].rearrange("p n r -> p (n r)").bitcast(I32))
-        n1_t = load_list("n1_t", n1)
         n2_t = load_list("n2_t", n2)
+        n1_t = load_list("n1_t", n1)
         n3_t = load_list("n3_t", n3)
         gain = held.tile([P, PACK], F32, name="gain")
         nc.sync.dma_start(gain[:], gs.rearrange("(p t) o -> p (t o)", t=PACK))
@@ -68,10 +69,10 @@ def tile_picked_ccmpclampbtrim_none_p_kernel(
         n6_t = load_list("n6_t", n6)
 
         last = PACK - 1
-        y_win = [held.tile([P, WINDOW if t < last else S], F32, name="y_win%d" % t) for t in range(PACK)]
+        y_win = [held.tile([P, WINDOW if t < last else S], F32, name="y_win%d" % t, tag="y_win%d" % t) for t in range(PACK)]
         a_win = [held.tile([P, WINDOW], F32, name="a_win%d" % t) for t in range(PACK)]
         b_win = [held.tile([P, WINDOW], F32, name="b_win%d" % t) for t in range(PACK)]
-        for t in range(last):
+        for t in range(2):
             nc.gpsimd.memset(y_win[t][:, spare(ALL)], 0.0)
 
         identity = held.tile([P, P], F32, name="identity")
@@ -137,19 +138,22 @@ def tile_picked_ccmpclampbtrim_none_p_kernel(
                 stop=True,
             )
 
+        y_own = [held.tile([P, S], F32, name="y_own%d" % t) for t in (2, 3)]
+        y_plain = [None, y_win[2][:, spare(ALL)], y_own[0][:], y_own[1][:]]
+
         def make_y(t, cols):
             bank = next_bank()
             product(bank, cols, w_codes, w_scales, t, xq_words, xq_scales)
             nc.scalar.activation(y_win[t][:, cols], bank[:, cols], COPY, scale=-1.0)
-            nc.scalar.activation(a_win[t][:, spare(cols)], bank[:, cols], COPY, scale=-1.0)
+            if t > 0:
+                nc.scalar.activation(y_plain[t][:, cols], bank[:, cols], COPY, scale=-1.0)
 
         make_y(0, first)
         make_y(0, second)
-        for t in range(1, PACK):
-            make_y(t, ALL)
+        make_y(1, ALL)
 
         third, fourth = slice(HALF, HALF + P), slice(HALF + P, S)
-        pair_sum = [held.tile([P, S], F32, name="pair_sum%d" % t, tag="pair_sum%d" % t) for t in range(PACK)]
+        pair_sum = [a_win[t][:, spare(ALL)] for t in range(PACK)]
         less2 = [held.tile([P, S], F32, name="less2_%d" % t) for t in range(PACK)]
         less3 = [held.tile([P, S], F32, name="less3_%d" % t) for t in range(PACK)]
         least = [held.tile([P, S], F32, name="least%d" % t, tag="least%d" % t, align_bytes=64) for t in range(PACK)]
@@ -159,7 +163,7 @@ def tile_picked_ccmpclampbtrim_none_p_kernel(
 
         def fetch1(t, cols):
             nc.vector.tensor_tensor(
-                pair_sum[t][:, cols], y_win[t][:].indirect(n1_t[:, entries(cols)]), a_win[t][:, spare(cols)], ALU.add
+                pair_sum[t][:, cols], y_win[t][:].indirect(n1_t[:, entries(cols)]), y_plain[t][:, cols], ALU.add
             )
 
         def fetch2(t, cols):
@@ -194,12 +198,27 @@ def tile_picked_ccmpclampbtrim_none_p_kernel(
             product(bank, ALL, cb_words, cb_scales, t, z_codes, z_scales)
             nc.scalar.activation(b_win[t][:, ALL], bank[:], COPY, scale=0.0625)
 
-        fetch1(0, ALL)
+        blocks = [slice(q, q + P) for q in range(0, S, P)]
+        nc.vector.tensor_copy(least[0][:], y_win[0][:].indirect(n2_t[:]))
+        nc.vector.tensor_tensor(less3[0][:], y_win[0][:].indirect(n3_t[:]), least[0][:], ALU.subtract)
         fetch1(1, ALL)
-        fetch2(0, ALL)
-        fetch3(0, ALL)
+        nc.vector.tensor_tensor(pair_sum[0], y_win[0][:].indirect(n1_t[:]), least[0][:], ALU.subtract)
+        nc.scalar.activation(less2[0][:], less3[0][:], RELU, scale=-1.0)
+        there = next_bank()
+        terms = [(src, blk) for src in (y_win[0][:, ALL], less2[0][:], pair_sum[0]) for blk in blocks]
+        for i, (src, blk) in enumerate(terms):
+            nc.tensor.matmul(
+                there[:, blk], src[:, blk], identity[:], start=(i == 0), stop=(i == len(terms) - 1), is_transpose=True
+            )
+        z_turned = held.tile([P, S], F32, name="z_turned")
+        nc.scalar.activation(z_turned[:], there[:], COPY, scale=-1.0)
+        back = next_bank()
+        for blk in blocks:
+            nc.tensor.transpose(back[:, blk], z_turned[:, blk], identity[:])
+        nc.scalar.activation(z_bf[:, :, 0], back[:], COPY, scale=gain[:, 0:1])
+        make_y(2, ALL)
+        make_y(3, ALL)
         fetch2(1, ALL)
-        make_z(0, ALL)
         fetch3(1, ALL)
         fetch1(2, ALL)
         make_z(1, ALL)
@@ -220,7 +239,7 @@ def tile_picked_ccmpclampbtrim_none_p_kernel(
         make_z(3, fourth)
         make_a(0, first)
         quantize_z(third)
-        cb_late = held.tile([P, HALF], U8, name="cb_late", tag="pair_sum%d" % last)
+        cb_late = held.tile([P, HALF], U8, name="cb_late", tag="y_win%d" % last)
         gather_scales(cb_late, cb_t, second)
         make_a(0, third)
         quantize_z(fourth)
@@ -258,9 +277,11 @@ def tile_picked_ccmpclampbtrim_none_p_kernel(
             )
             blocks = [slice(q, q + P) for q in range(cols.start, cols.stop, P)]
             there = next_bank()
-            for blk in blocks:
-                nc.tensor.matmul(there[:, blk], trimmed[t][:, blk], identity[:], start=True, stop=False, is_transpose=True)
-                nc.tensor.matmul(there[:, blk], capped[t][:, blk], identity[:], start=False, stop=True, is_transpose=True)
+            terms = [(src, blk) for src in (trimmed[t], capped[t]) for blk in blocks]
+            for i, (src, blk) in enumerate(terms):
+                nc.tensor.matmul(
+                    there[:, blk], src[:, blk], identity[:], start=(i == 0), stop=(i == len(terms) - 1), is_transpose=True
+                )
             nc.scalar.copy(turned[t][:, cols], there[:, cols])
             back = next_bank()
             for blk in blocks:

@@ -199,8 +199,12 @@ def tile_picked_ccmpclampbtrim_none_p_kernel(
             nc.scalar.activation(b_win[t][:, ALL], bank[:], COPY, scale=0.0625)
 
         blocks = [slice(q, q + P) for q in range(0, S, P)]
-        nc.vector.tensor_copy(least[0][:], y_win[0][:].indirect(n2_t[:]))
-        nc.vector.tensor_tensor(less3[0][:], y_win[0][:].indirect(n3_t[:]), least[0][:], ALU.subtract)
+        for cols in HALVES:
+            nc.vector.tensor_copy(least[0][:, cols], y_win[0][:].indirect(n2_t[:, entries(cols)]))
+        for cols in HALVES:
+            nc.vector.tensor_tensor(
+                less3[0][:, cols], y_win[0][:].indirect(n3_t[:, entries(cols)]), least[0][:, cols], ALU.subtract
+            )
         fetch1(1, ALL)
         nc.vector.tensor_tensor(pair_sum[0], y_win[0][:].indirect(n1_t[:]), least[0][:], ALU.subtract)
         nc.scalar.activation(less2[0][:], less3[0][:], RELU, scale=-1.0)
@@ -312,6 +316,6 @@ def tile_picked_ccmpclampbtrim_none_p_kernel(
             fetch(upper, n5_t, cols)
         for cols in HALVES:
             nc.vector.tensor_tensor(capped[last][:, cols], trimmed[last][:, cols], upper[last][:, cols], ALU.min)
-        for cols in HALVES:
+        for cols in (first, third, fourth):
             nc.vector.tensor_tensor(result[last][:, cols], capped[last][:, cols], lower[last][:, cols], ALU.max)
             nc.sync.dma_start(out_rows[last][:, :, cols], result[last][:, cols])

from contextlib import ExitStack

import concourse.mybir as mybir
from concourse.masks import make_identity

K, T, S, H, C = 512, 2048, 512, 512, 512
FLOPS = 2 * K * S * (H + 2 * C)

F32 = mybir.dt.float32
BF16 = mybir.dt.bfloat16
I32 = mybir.dt.int32
U32 = mybir.dt.uint32
U16 = mybir.dt.uint16
U8 = mybir.dt.uint8
FP8X4 = mybir.dt.float8_e4m3fn_x4
ALU = mybir.AluOpType
RELU = mybir.ActivationFunctionType.Relu
COPY = mybir.ActivationFunctionType.Copy

P = 128
PACK = 4
HALF = S // 2
WINDOW = 2 * S
ALL = slice(0, S)
HALVES = (slice(0, HALF), slice(HALF, S))


def entries(cols):
    return slice(cols.start // 16, cols.stop // 16)


def spare(cols):
    return slice(S + cols.start, S + cols.stop)


def tile_picked_ccmpclampbtrim_none_p_kernel(
    tc, x_words, x_scales, w1, gs, offs, n1, n2, n3, ca, cb, n4, n5, n6, out
):
    nc = tc.nc
    with ExitStack() as ctx:
        held = ctx.enter_context(tc.tile_pool(name="held", bufs=1))
        psum = ctx.enter_context(tc.psum_pool(name="psum", bufs=1))

        def load_list(name, src):
            tile = held.tile([P, S // 16], U16, name=name)
            nc.sync.dma_start(tile[:], src)
            return tile

        table_scales = held.tile([P, T], U8, name="table_scales")
        nc.gpsimd.memset(table_scales[:].bitcast(I32), 0)
        offs_t = load_list("offs_t", offs)
        ca_t = load_list("ca_t", ca)
        cb_t = load_list("cb_t", cb)
        for q in range(4):
            nc.sync.dma_start(
                table_scales[q:P:32, :].bitcast(I32), x_scales[0, q:16:4, :].bitcast(I32)
            )
        w_raw = held.tile([P, PACK, H], F32, name="w_raw")
        nc.sync.dma_start(w_raw[:], w1.rearrange("(p j) c -> p j c", j=PACK))
        table_words = held.tile([P, T], U32, name="table_words")
        nc.sync.dma_start(table_words[:].bitcast(I32), x_words[0].rearrange("p n r -> p (n r)").bitcast(I32))
        n2_t = load_list("n2_t", n2)
        n1_t = load_list("n1_t", n1)
        n3_t = load_list("n3_t", n3)
        gain = held.tile([P, PACK], F32, name="gain")
        nc.sync.dma_start(gain[:], gs.rearrange("(p t) o -> p (t o)", t=PACK))
        n4_t = load_list("n4_t", n4)
        n5_t = load_list("n5_t", n5)
        n6_t = load_list("n6_t", n6)

        last = PACK - 1
        y_win = [held.tile([P, WINDOW if t < last else S], F32, name="y_win%d" % t, tag="y_win%d" % t) for t in range(PACK)]
        a_win = [held.tile([P, WINDOW], F32, name="a_win%d" % t) for t in range(PACK)]
        b_win = [held.tile([P, WINDOW], F32, name="b_win%d" % t) for t in range(PACK)]
        for t in range(2):
            nc.gpsimd.memset(y_win[t][:, spare(ALL)], 0.0)

        identity = held.tile([P, P], F32, name="identity")
        make_identity(nc, identity[:])

        def gather_scales(tile, lst, cols):
            nc.vector.tensor_copy(tile[:], table_scales[:].indirect(lst[:, entries(cols)]))

        def deal_scales(tile, cols, src):
            nc.vector.tensor_copy(
                tile[:].bitcast(I32).rearrange("p (t c) -> p t c", t=PACK)[:, :, entries(cols)],
                src[:].bitcast(I32).rearrange("p (c t) -> p t c", t=PACK),
            )

        def gather_dealt_words(tile, lst):
            nc.vector.tensor_copy(
                tile[:].rearrange("p (t c b) -> p c t b", t=PACK, b=4), table_words[:].indirect(lst[:])
            )

        first, second = HALVES
        xq_scales = held.tile([P, S], U8, name="xq_scales", align_bytes=64)
        gather_scales(xq_scales, offs_t, ALL)
        ca_plain = held.tile([P, C], U8, name="ca_plain")
        gather_scales(ca_plain, ca_t, ALL)
        cb_early = held.tile([P, HALF], U8, name="cb_early")
        gather_scales(cb_early, cb_t, first)
        ca_scales = held.tile([P, C], U8, name="ca_scales", align_bytes=64)
        cb_scales = held.tile([P, C], U8, name="cb_scales", align_bytes=64)
        deal_scales(ca_scales, ALL, ca_plain)
        deal_scales(cb_scales, first, cb_early)

        raw_view = w_raw[:].rearrange("p j (m t) -> p m t j", t=PACK)
        w_codes = held.tile([P, H], U32, name="w_codes", align_bytes=64)
        w_scales = held.tile([P, H], U8, name="w_scales", align_bytes=64)
        w_bf = [held.tile([P, 2 * H], BF16, name="w_bf%d" % u, tag="w_bf%d" % u, align_bytes=64) for u in range(2)]
        w_view = [tile[:].rearrange("p (t m j) -> p m t j", t=2, j=PACK) for tile in w_bf]
        nc.scalar.copy(w_view[0], raw_view[:, :, 0:2])
        nc.scalar.copy(w_view[1], raw_view[:, :, 2:4])
        for u, cols in enumerate(HALVES):
            nc.vector.quantize_mx(out=w_codes[:, cols].bitcast(FP8X4), scales=w_scales[:, cols], in_=w_bf[u][:])

        xq_words = held.tile([P, S], U32, name="xq_words", tag="w_bf0", align_bytes=64)
        for cols in HALVES:
            nc.vector.tensor_copy(xq_words[:, cols], table_words[:].indirect(offs_t[:, entries(cols)]))
        ca_words = held.tile([P, C], U32, name="ca_words", tag="w_bf1", align_bytes=64)
        gather_dealt_words(ca_words, ca_t)

        turn = [0]

        def next_bank():
            turn.append(turn[-1] + 1)
            return psum.tile([P, S], F32, name="bank%d" % turn[-1], tag="bank%d" % (turn[-1] % 8))

        def product(bank, cols, left_words, left_scales, t, right_words, right_scales):
            rows = slice(P * t, P * (t + 1))
            nc.tensor.matmul_mx(
                out=bank[:, cols],
                lhsT=left_words[:, rows].bitcast(FP8X4),
                lhsT_scale=left_scales[:, rows],
                rhs=right_words[:, cols].bitcast(FP8X4),
                rhs_scale=right_scales[:, cols],
                start=True,
                stop=True,
            )

        y_own = [held.tile([P, S], F32, name="y_own%d" % t) for t in (2, 3)]
        y_plain = [None, y_win[2][:, spare(ALL)], y_own[0][:], y_own[1][:]]

        def make_y(t, cols):
            bank = next_bank()
            product(bank, cols, w_codes, w_scales, t, xq_words, xq_scales)
            nc.scalar.activation(y_win[t][:, cols], bank[:, cols], COPY, scale=-1.0)
            if t > 0:
                nc.scalar.activation(y_plain[t][:, cols], bank[:, cols], COPY, scale=-1.0)

        make_y(0, first)
        make_y(0, second)
        make_y(1, ALL)

        third, fourth = slice(HALF, HALF + P), slice(HALF + P, S)
        pair_sum = [a_win[t][:, spare(ALL)] for t in range(PACK)]
        less2 = [held.tile([P, S], F32, name="less2_%d" % t) for t in range(PACK)]
        less3 = [held.tile([P, S], F32, name="less3_%d" % t) for t in range(PACK)]
        least = [held.tile([P, S], F32, name="least%d" % t, tag="least%d" % t, align_bytes=64) for t in range(PACK)]
        z_bf = held.tile([P, S, PACK], BF16, name="z_bf", align_bytes=64)
        z_codes = held.tile([P, S], U32, name="z_codes", align_bytes=64)
        z_scales = held.tile([P, S], U8, name="z_scales", align_bytes=64)

        def fetch1(t, cols):
            nc.vector.tensor_tensor(
                pair_sum[t][:, cols], y_win[t][:].indirect(n1_t[:, entries(cols)]), y_plain[t][:, cols], ALU.add
            )

        def fetch2(t, cols):
            nc.vector.tensor_tensor(
                less2[t][:, cols], y_win[t][:].indirect(n2_t[:, entries(cols)]), pair_sum[t][:, cols], ALU.subtract
            )

        def fetch3(t, cols):
            nc.vector.tensor_tensor(
                less3[t][:, cols], y_win[t][:].indirect(n3_t[:, entries(cols)]), pair_sum[t][:, cols], ALU.subtract
            )

        def make_z(t, cols):
            nc.vector.tensor_tensor(least[t][:, cols], less2[t][:, cols], less3[t][:, cols], ALU.min)
            nc.scalar.activation(z_bf[:, cols, t], least[t][:, cols], COPY, scale=gain[:, t : t + 1])

        def quantize_z(cols):
            nc.vector.quantize_mx(
                out=z_codes[:, cols].bitcast(FP8X4),
                scales=z_scales[:, cols],
                in_=z_bf[:, cols, :].rearrange("p c t -> p (c t)"),
            )

        def make_a(t, cols):
            bank = next_bank()
            product(bank, cols, ca_words, ca_scales, t, z_codes, z_scales)
            nc.scalar.activation(a_win[t][:, cols], bank[:, cols], COPY, scale=-0.03125)
            nc.scalar.activation(b_win[t][:, spare(cols)], bank[:, cols], COPY, scale=0.0625)

        def make_b(t):
            bank = next_bank()
            product(bank, ALL, cb_words, cb_scales, t, z_codes, z_scales)
            nc.scalar.activation(b_win[t][:, ALL], bank[:], COPY, scale=0.0625)

        blocks = [slice(q, q + P) for q in range(0, S, P)]
        for cols in HALVES:
            nc.vector.tensor_copy(least[0][:, cols], y_win[0][:].indirect(n2_t[:, entries(cols)]))
        for cols in HALVES:
            nc.vector.tensor_tensor(
                less3[0][:, cols], y_win[0][:].indirect(n3_t[:, entries(cols)]), least[0][:, cols], ALU.subtract
            )
        fetch1(1, ALL)
        nc.vector.tensor_tensor(pair_sum[0], y_win[0][:].indirect(n1_t[:]), least[0][:], ALU.subtract)
        nc.scalar.activation(less2[0][:], less3[0][:], RELU, scale=-1.0)
        there = next_bank()
        terms = [(src, blk) for src in (y_win[0][:, ALL], less2[0][:], pair_sum[0]) for blk in blocks]
        for i, (src, blk) in enumerate(terms):
            nc.tensor.matmul(
                there[:, blk], src[:, blk], identity[:], start=(i == 0), stop=(i == len(terms) - 1), is_transpose=True
            )
        z_turned = held.tile([P, S], F32, name="z_turned")
        nc.scalar.activation(z_turned[:], there[:], COPY, scale=-1.0)
        back = next_bank()
        for blk in blocks:
            nc.tensor.transpose(back[:, blk], z_turned[:, blk], identity[:])
        nc.scalar.activation(z_bf[:, :, 0], back[:], COPY, scale=gain[:, 0:1])
        make_y(2, ALL)
        make_y(3, ALL)
        fetch2(1, ALL)
        fetch3(1, ALL)
        fetch1(2, ALL)
        make_z(1, ALL)
        fetch2(2, ALL)
        fetch1(3, first)
        fetch3(2, ALL)
        fetch1(3, second)
        make_z(2, ALL)
        fetch2(3, first)
        fetch3(3, first)
        fetch2(3, third)
        make_z(3, first)
        fetch3(3, third)
        fetch2(3, fourth)
        make_z(3, third)
        fetch3(3, fourth)
        quantize_z(first)
        make_z(3, fourth)
        make_a(0, first)
        quantize_z(third)
        cb_late = held.tile([P, HALF], U8, name="cb_late", tag="y_win%d" % last)
        gather_scales(cb_late, cb_t, second)
        make_a(0, third)
        quantize_z(fourth)
        cb_words = held.tile([P, C], U32, name="cb_words", tag="least%d" % last, align_bytes=64)
        gather_dealt_words(cb_words, cb_t)
        deal_scales(cb_scales, second, cb_late)

        make_a(0, fourth)
        make_a(1, ALL)
        make_b(0)
        make_b(1)
        for t in range(2, PACK):
            make_a(t, ALL)
            make_b(t)

        trimmed = [held.tile([P, S], F32, name="trimmed%d" % t) for t in range(PACK)]
        upper = [held.tile([P, S], F32, name="upper%d" % t) for t in range(PACK)]
        lower = [held.tile([P, S], F32, name="lower%d" % t) for t in range(PACK)]
        capped = [held.tile([P, S], F32, name="capped%d" % t) for t in range(PACK)]
        turned = [held.tile([P, S], F32, name="turned%d" % t) for t in range(last)]
        result = [held.tile([P, S], F32, name="result%d" % t) for t in range(PACK)]
        out_rows = out.rearrange("(c t b) j -> t c b j", t=PACK, b=4)

        def fetch4(t):
            nc.vector.tensor_tensor(trimmed[t][:], a_win[t][:].indirect(n4_t[:]), b_win[t][:, spare(ALL)], ALU.add)

        def room(t, dst, lst, cols):
            nc.vector.tensor_tensor(
                dst[t][:, cols], b_win[t][:].indirect(lst[:, entries(cols)]), trimmed[t][:, cols], ALU.subtract
            )

        def shift_and_store(t, cols):
            nc.vector.scalar_tensor_tensor(
                capped[t][:, cols], upper[t][:, cols], 0.0, lower[t][:, cols], ALU.min, ALU.max
            )
            blocks = [slice(q, q + P) for q in range(cols.start, cols.stop, P)]
            there = next_bank()
            terms = [(src, blk) for src in (trimmed[t], capped[t]) for blk in blocks]
            for i, (src, blk) in enumerate(terms):
                nc.tensor.matmul(
                    there[:, blk], src[:, blk], identity[:], start=(i == 0), stop=(i == len(terms) - 1), is_transpose=True
                )
            nc.scalar.copy(turned[t][:, cols], there[:, cols])
            back = next_bank()
            for blk in blocks:
                nc.tensor.transpose(back[:, blk], turned[t][:, blk], identity[:])
            nc.scalar.copy(result[t][:, cols], back[:, cols])
            nc.scalar.dma_start(out_rows[t][:, :, cols], result[t][:, cols])

        def fetch(dst, lst, cols):
            nc.vector.tensor_copy(dst[last][:, cols], b_win[last][:].indirect(lst[:, entries(cols)]))

        fetch4(0)
        fetch4(1)
        room(0, upper, n5_t, ALL)
        room(0, lower, n6_t, ALL)
        room(1, upper, n5_t, ALL)
        shift_and_store(0, ALL)
        room(1, lower, n6_t, ALL)
        fetch4(2)
        shift_and_store(1, ALL)
        room(2, upper, n5_t, ALL)
        for cols in HALVES:
            room(2, lower, n6_t, cols)
        for cols in HALVES:
            shift_and_store(2, cols)
        fetch4(last)
        fetch(lower, n6_t, ALL)
        for cols in HALVES:
            fetch(upper, n5_t, cols)
        for cols in HALVES:
            nc.vector.tensor_tensor(capped[last][:, cols], trimmed[last][:, cols], upper[last][:, cols], ALU.min)
        for cols in (first, third, fourth):
            nc.vector.tensor_tensor(result[last][:, cols], capped[last][:, cols], lower[last][:, cols], ALU.max)
            nc.sync.dma_start(out_rows[last][:, :, cols], result[last][:, cols])
